import numpy as np
import ml_dtypes


def mxq(x, axis, fmt="e4m3"):
    dtype, down = {"e4m3": (ml_dtypes.float8_e4m3fn, 7), "e5m2": (ml_dtypes.float8_e5m2, 14)}[fmt]
    v = np.moveaxis(np.asarray(x, np.float32).astype(ml_dtypes.bfloat16).astype(np.float64), axis, -1)
    blocks = v.reshape(v.shape[:-1] + (-1, 32))
    amax = np.abs(blocks).max(-1, keepdims=True)
    byte = np.maximum(np.where(amax > 0, np.frexp(amax)[1] - 1 + 127, 0) - down, 1)
    scale = np.exp2(byte - 127.0)
    codes = (blocks / scale).astype(np.float32).astype(dtype).astype(np.float64)
    return np.moveaxis((codes * scale).reshape(v.shape), -1, axis)


WIDE = False


def mx_kscale(k):
    if not WIDE:
        return np.ones(k)
    levels = np.array([30, -30])
    if k % 512:
        return np.exp2(np.random.permutation(np.resize(levels, k // 32))).repeat(32)
    a = np.empty((k // 512, 16))
    for p in range(k // 512):
        a[p, :8] = np.random.permutation(np.resize(levels, 8))
        for g in range(8):
            far = levels[np.abs(levels - a[p, g]) >= 10]
            a[p, g + 8] = far[np.random.randint(len(far))]
    return np.exp2(a.ravel()).repeat(32)


def f64(x):
    return np.asarray(x).astype(np.float64)


def striped(idx):
    return np.tile(np.asarray(idx).reshape(-1, 16).T, (8, 1)).astype(np.uint16)


def unstriped(offs):
    return offs[:16].T.reshape(-1).astype(np.int64)


def striped8(idx):
    return np.asarray(idx).reshape(8, -1, 16).transpose(0, 2, 1).reshape(128, -1).astype(np.uint16)


def unstriped8(offs):
    return offs.reshape(8, 16, -1).transpose(0, 2, 1).reshape(8, -1).astype(np.int64)


def pick8(x, idx, run):
    r = np.arange(len(x))
    return x[r[:, None], idx[r % (8 * run) // run]]


E2M1 = np.array([0.0, 0.5, 1.0, 1.5, 2.0, 3.0, 4.0, 6.0, -0.0, -0.5, -1.0, -1.5, -2.0, -3.0, -4.0, -6.0])


def pack_weight(w, fmt):
    k, n = w.shape
    w = f64(np.asarray(w, np.float32).astype(ml_dtypes.bfloat16)).reshape(k // 32, 32, n)
    amax = np.abs(w).max(1)
    if fmt in ("e4m3", "e5m2"):
        byte = np.frexp(amax)[1] - 1 + 127 - (7 if fmt == "e4m3" else 14)
    else:
        mant, ex = np.frexp(amax / 6.0)
        byte = np.where(mant > 0.5, ex, ex - 1) + 127
    byte = np.clip(np.where(amax > 0, byte, 1), 1, 254)
    scaled = (w * np.exp2(127.0 - byte)[:, None, :]).reshape(k, n).astype(np.float32)
    by_word = np.ascontiguousarray(scaled.reshape(k // 512, 128, 4, n).transpose(0, 1, 3, 2))
    if fmt in ("e4m3", "e5m2"):
        words = by_word.astype(ml_dtypes.float8_e4m3fn if fmt == "e4m3" else ml_dtypes.float8_e5m2).view(np.uint8)
    else:
        c = by_word.astype(ml_dtypes.float4_e2m1fn).view(np.uint8) & 0xF
        words = (c[..., 0::2] | (c[..., 1::2] << 4)).reshape(k // 512, 128, 2 * n)
    return np.ascontiguousarray(words), np.ascontiguousarray(byte.astype(np.uint8).reshape(k // 512, 16, n))


def unpack_weight(words, scales, fmt):
    g, _, n = scales.shape
    words = np.ascontiguousarray(words).reshape(g, 128, n, -1)
    if fmt in ("e4m3", "e5m2"):
        vals = words.view(ml_dtypes.float8_e4m3fn if fmt == "e4m3" else ml_dtypes.float8_e5m2).astype(np.float64)
    else:
        nib = np.empty((g, 128, n, 4), np.uint8)
        nib[..., 0::2] = words & 0xF
        nib[..., 1::2] = words >> 4
        vals = E2M1[nib]
    vals = vals * np.repeat(np.exp2(scales.astype(np.float64) - 127.0), 8, axis=1)[..., None]
    return vals.transpose(0, 1, 3, 2).reshape(g * 512, n)


def bf(x):
    return np.asarray(x, np.float32).astype(ml_dtypes.bfloat16)


def planes(Y):
    r, m = Y.shape
    b = f64(bf(Y)).reshape(r // 32, 32, m)
    amax = np.abs(b).max(1)
    byte = np.clip(np.where(amax > 0, np.frexp(amax)[1] - 1 + 127 - 7, 1), 1, 254)
    codes = (b * np.exp2(127.0 - byte)[:, None, :]).reshape(r, m).astype(np.float32).astype(ml_dtypes.float8_e4m3fn).view(np.uint8)
    words = codes.reshape(r // 512, 128, 4, m).transpose(0, 1, 3, 2)
    return np.ascontiguousarray(words), np.ascontiguousarray(byte.astype(np.uint8).reshape(r // 512, 16, m))


K, T, J, R, C, O, N, D = 512, 512, 256, 512, 1024, 256, 512, 1024


def setup_inputs():
    n = np.random.standard_normal
    idx = np.stack([np.random.permutation(T)[:J] for _ in range(8)])
    idx2 = np.random.permutation(C)[:J]
    idx3 = np.random.permutation(C)[:O]
    idx4 = np.random.permutation(D)[:O]
    fk = mx_kscale(K)
    fr = mx_kscale(R)
    xtp = pack_weight(n((K, T)) / fk[:, None], "e4m3")
    wp = pack_weight(n((K, R)) * 1 / np.sqrt(K) * fk[:, None] * fr, "e5m2")
    wbp = pack_weight(n((R, N)) * 1 / np.sqrt(R) / fr[:, None], "e2m1")
    return {
        "xt_words": xtp[0],
        "xt_scales": xtp[1],
        "w_words": wp[0],
        "w_scales": wp[1],
        "oldh": (n((R, C)) * 0.7 * fr[:, None]).astype(np.float32),
        "wb_words": wbp[0],
        "wb_scales": wbp[1],
        "old": (1.0 * n((N, C))).astype(np.float32),
        "offs": striped8(idx),
        "offs2": striped(idx2),
        "offs3": striped(idx3),
        "offs4": striped(idx4),
    }


def reference(xt_words, xt_scales, w_words, w_scales, oldh, wb_words, wb_scales, old, offs, offs2, offs3, offs4):
    idx = unstriped8(offs)
    idx2 = unstriped(offs2)
    idx3 = unstriped(offs3)
    idx4 = unstriped(offs4)
    xtu = unpack_weight(xt_words, xt_scales, "e4m3")
    wu = unpack_weight(w_words, w_scales, "e5m2")
    wbu = unpack_weight(wb_words, wb_scales, "e2m1")
    xtidxg = pick8(xtu, idx, 64)
    a = wu.T @ xtidxg
    ha = np.maximum(a, 0.0)
    pw0 = np.zeros((R, C))
    pw0[:, idx2] = ha
    pg = pw0 + f64(oldh)
    hid = pg[:, idx3]
    hidq = mxq(hid, 0, "e5m2")
    p = wbu.T @ hidq
    pp = np.zeros((N, D))
    pp[:, idx4] = p
    y = pp + 0.5 * f64(old)
    words, scales = planes(y)
    return y, words, scales

@@ -1,0 +1,200 @@
+from contextlib import ExitStack
+
+import concourse.mybir as mybir
+
+K, T, J, R, C, O, N, D = 512, 512, 256, 512, 1024, 256, 512, 1024
+FLOPS = 2 * K * R * J + 2 * R * N * O
+
+F32 = mybir.dt.float32
+BF16 = mybir.dt.bfloat16
+I32 = mybir.dt.int32
+U32 = mybir.dt.uint32
+U16 = mybir.dt.uint16
+U8 = mybir.dt.uint8
+E4M3 = mybir.dt.float8_e4m3fn_x4
+E5M2 = mybir.dt.float8_e5m2_x4
+E2M1 = mybir.dt.float4_e2m1fn_x4
+ACT = mybir.ActivationFunctionType
+ALU = mybir.AluOpType
+
+P = 128
+PACK = 4
+ALIGN = 64
+HALF = D // 2
+ON_VECTOR = 1
+
+
+def tile_list_page_headpicks_scattered_pl_kernel(
+    tc, xt_words, xt_scales, w_words, w_scales, oldh, wb_words, wb_scales, old, offs, offs2, offs3, offs4, out_0, out_1, out_2
+):
+    nc = tc.nc
+    with ExitStack() as ctx:
+        lists = ctx.enter_context(tc.tile_pool(name="lists", bufs=1))
+        sb = ctx.enter_context(tc.tile_pool(name="sb", bufs=1))
+        psum = ctx.enter_context(tc.psum_pool(name="psum", bufs=1))
+
+        def tile(shape, dtype, name, tag=None):
+            return sb.tile(shape, dtype, name=name, tag=tag or name, align_bytes=ALIGN)
+
+        pick = lists.tile([P, J // 16], U16, name="pick")
+        put_h = lists.tile([P, J // 16], U16, name="put_h")
+        read_h = lists.tile([P, O // 16], U16, name="read_h")
+        put_y = lists.tile([P, O // 16], U16, name="put_y")
+
+        xs_raw = tile([P, T], U8, "xs_raw")
+        ws_raw = tile([P, R + N], U8, "ws_raw")
+        planes = tile([P, R + J + N], U8, "planes")
+        nc.vector.memset(xs_raw[:].bitcast(I32), 0)
+        nc.vector.memset(ws_raw[:].bitcast(I32), 0)
+        nc.vector.memset(planes[:].bitcast(I32), 0)
+
+        xw_raw = tile([P, T], I32, "xw_raw")
+        ww_raw = tile([P, R], I32, "ww_raw")
+        wbw_raw = tile([P, 2 * N], U8, "wbw_raw", tag="page2")
+        nc.sync.dma_start(pick[:], offs)
+        nc.scalar.dma_start(xs_raw[0:P:8, :].bitcast(I32), xt_scales[0].bitcast(I32))
+        nc.scalar.dma_start(ws_raw[0:P:8, 0:R].bitcast(I32), w_scales[0].bitcast(I32))
+        nc.sync.dma_start(xw_raw[:], xt_words[0].rearrange("p c r -> p (c r)").bitcast(I32))
+        nc.sync.dma_start(ww_raw[:], w_words[0].rearrange("p c r -> p (c r)").bitcast(I32))
+        nc.sync.dma_start(put_h[:], offs2)
+        nc.sync.dma_start(read_h[:], offs3)
+        nc.sync.dma_start(put_y[:], offs4)
+        nc.sync.dma_start(wbw_raw[:].bitcast(I32), wb_words[0].bitcast(I32))
+        nc.scalar.dma_start(ws_raw[0:P:8, R : R + N].bitcast(I32), wb_scales[0].bitcast(I32))
+
+        placed_h = [None] * PACK
+        for t in range(2):
+            placed_h[t] = tile([P, C], F32, "placed_h%d" % t)
+            nc.vector.memset(placed_h[t][:], 0.0)
+
+        xs_picked = tile([P, J], U8, "xs_picked")
+        nc.vector.tensor_copy(xs_picked[:], xs_raw[:].indirect(pick[:]))
+        spread = tile([P, R + J], U8, "spread", tag="oldh")
+        nc.vector.tensor_copy(
+            spread[:, 0:R].rearrange("p (t m) -> p t m", t=PACK), ws_raw[:, 0:R].rearrange("p (m t) -> p t m", t=PACK)
+        )
+        nc.vector.tensor_copy(spread[:, R : R + J].bitcast(I32), xs_picked[:].bitcast(I32))
+        for x in range(4):
+            queue = nc.scalar if x % 2 == 0 else nc.sync
+            queue.dma_start(planes[32 * x : 32 * x + 4, 0 : R + J].bitcast(I32), spread[32 * x : 32 * x + 32 : 8, :].bitcast(I32))
+
+        xw = tile([P, J], I32, "xw", tag="page3")
+        nc.vector.tensor_copy(xw[:].bitcast(U32), xw_raw[:].bitcast(U32).indirect(pick[:]))
+        ww = tile([P, R], I32, "ww", tag="old")
+        nc.vector.tensor_copy(
+            ww[:].rearrange("p (t c i) -> p c t i", t=PACK, i=4), ww_raw[:].rearrange("p (c i t) -> p c t i", t=PACK, i=4)
+        )
+        spread_b = tile([P, N], U8, "spread_b")
+        nc.vector.tensor_copy(
+            spread_b[:].rearrange("p (t m) -> p t m", t=PACK), ws_raw[:, R : R + N].rearrange("p (m t) -> p t m", t=PACK)
+        )
+        wbw = tile([P, 2 * N], U8, "wbw")
+        nc.vector.tensor_copy(
+            wbw[:].rearrange("p (t m b) -> p t m b", t=PACK, b=2), wbw_raw[:].rearrange("p (m t b) -> p t m b", t=PACK, b=2)
+        )
+
+        oldh_sb = tile([P, PACK, C], F32, "oldh_sb", tag="oldh")
+        oldh_rows = oldh.rearrange("(p t) c -> p t c", t=PACK)
+        for t in range(PACK):
+            nc.sync.dma_start(oldh_sb[:, t, :], oldh_rows[:, t, :])
+        for x in range(4):
+            nc.sync.dma_start(
+                planes[32 * x : 32 * x + 4, R + J : R + J + N].bitcast(I32), spread_b[32 * x : 32 * x + 32 : 8, :].bitcast(I32)
+            )
+
+        a = [psum.tile([P, J], F32, name="a%d" % t) for t in range(PACK)]
+        for t in range(PACK):
+            cols = slice(t * P, (t + 1) * P)
+            nc.tensor.matmul_mx(
+                a[t][:], lhsT=ww[:, cols].bitcast(E5M2), lhsT_scale=planes[:, cols],
+                rhs=xw[:].bitcast(E4M3), rhs_scale=planes[:, R : R + J], start=True, stop=True,
+            )
+
+        old_sb = tile([P, PACK, D], F32, "old_sb", tag="old")
+        old_rows = old.rearrange("(p t) d -> p t d", t=PACK)
+        for u in range(2):
+            nc.sync.dma_start(old_sb[:, 2 * u : 2 * u + 2, :], old_rows[:, 2 * u : 2 * u + 2, :])
+        for t in range(2, PACK):
+            placed_h[t] = tile([P, C], F32, "placed_h%d" % t, tag="page%d" % t)
+            nc.gpsimd.memset(placed_h[t][:], 0.0)
+
+        def scatter(t, window, offsets, values):
+            if t == ON_VECTOR:
+                nc.vector.tensor_copy(window[:].indirect(offsets[:]), values[:])
+            else:
+                nc.scalar.activation(window[:].indirect(offsets[:]), values[:], ACT.Copy)
+
+        ha = [tile([P, J], F32, "ha%d" % t, tag="ha%d" % t) for t in range(PACK)]
+        for t in range(PACK):
+            if t % 2 == 0:
+                nc.scalar.activation(ha[t][:], a[t][:], ACT.Relu)
+            else:
+                nc.vector.tensor_scalar_max(ha[t][:], a[t][:], 0.0)
+        for t in range(PACK):
+            scatter(t, placed_h[t], put_h, ha[t])
+        placed_y = []
+        for t in range(PACK):
+            placed_y.append(tile([P, D], F32, "placed_y%d" % t, tag="ha%d" % t))
+            nc.gpsimd.memset(placed_y[t][:], 0.0)
+        pg = [tile([P, C], F32, "pg%d" % t) for t in range(PACK)]
+        for t in range(PACK):
+            nc.vector.tensor_tensor(pg[t][:], placed_h[t][:], oldh_sb[:, t, :], ALU.add)
+        hid = tile([P, PACK, O], BF16, "hid")
+        for t in range(PACK):
+            if t == PACK - 1:
+                nc.vector.tensor_copy(hid[:, t, :], pg[t][:].indirect(read_h[:]))
+            else:
+                nc.scalar.activation(hid[:, t, :], pg[t][:].indirect(read_h[:]), ACT.Copy)
+        hid_grouped = tile([P, O, PACK], BF16, "hid_grouped")
+        nc.vector.tensor_copy(
+            hid_grouped[:].rearrange("p (c i) t -> p c t i", i=4), hid[:].rearrange("p t (c i) -> p c t i", i=4)
+        )
+        hid_codes = tile([P, O], U32, "hid_codes")
+        hid_scales = tile([P, O], U8, "hid_scales")
+        nc.vector.quantize_mx(hid_codes[:].bitcast(E5M2), hid_scales[:], hid_grouped[:].rearrange("p o t -> p (o t)"))
+
+        prod = [psum.tile([P, O], F32, name="prod%d" % t) for t in range(PACK)]
+        for t in range(PACK):
+            nc.tensor.matmul_mx(
+                prod[t][:], lhsT=wbw[:, 2 * P * t : 2 * P * (t + 1)].bitcast(E2M1),
+                lhsT_scale=planes[:, R + J + P * t : R + J + P * (t + 1)],
+                rhs=hid_codes[:].bitcast(E5M2), rhs_scale=hid_scales[:], start=True, stop=True,
+            )
+        p_sb = [tile([P, O], F32, "p_sb%d" % t) for t in range(PACK)]
+        for t in range(PACK):
+            if t % 2 == 0:
+                nc.scalar.activation(p_sb[t][:], prod[t][:], ACT.Copy)
+            else:
+                nc.vector.tensor_copy(p_sb[t][:], prod[t][:])
+        for t in range(PACK):
+            scatter(t, placed_y[t], put_y, p_sb[t])
+
+        y = tile([P, PACK, D], F32, "y")
+        y_rows = out_0.rearrange("(p t) d -> p t d", t=PACK)
+        for t in range(PACK):
+            pieces = [slice(0, HALF), slice(HALF, D)] if t == PACK - 1 else [slice(0, D)]
+            for cols in pieces:
+                nc.vector.scalar_tensor_tensor(y[:, t, cols], old_sb[:, t, cols], 0.5, placed_y[t][:, cols], ALU.mult, ALU.add)
+            nc.sync.dma_start(y_rows[:, t, :], y[:, t, :])
+
+        y_grouped = tile([P, D, PACK], BF16, "y_grouped")
+        y_codes = tile([P, D], U32, "y_codes")
+        y_scales = tile([P, D], U8, "y_scales")
+        words_out = out_1[0].rearrange("p c r -> p (c r)").bitcast(I32)
+        for half in range(2):
+            cols = slice(half * HALF, (half + 1) * HALF)
+            dst = y_grouped[:, cols, :].rearrange("p (c i) t -> p c t i", i=4)
+            src = y[:, :, cols].rearrange("p t (c i) -> p c t i", i=4)
+            if half == 0:
+                nc.scalar.activation(dst, src, ACT.Copy)
+            else:
+                nc.vector.tensor_copy(dst, src)
+        for half in (1, 0):
+            cols = slice(half * HALF, (half + 1) * HALF)
+            nc.vector.quantize_mx(
+                y_codes[:, cols].bitcast(E4M3), y_scales[:, cols], y_grouped[:, cols, :].rearrange("p c t -> p (c t)")
+            )
+            nc.sync.dma_start(words_out[:, cols], y_codes[:, cols].bitcast(I32))
+        for x in range(4):
+            queue = nc.scalar if x % 2 == 0 else nc.sync
+            queue.dma_start(out_2[0, 4 * x : 4 * x + 4, :].bitcast(I32), y_scales[32 * x : 32 * x + 4, :].bitcast(I32))

@@ -20,7 +20,6 @@ ALU = mybir.AluOpType
 P = 128
 PACK = 4
 ALIGN = 64
-HALF = D // 2
 ON_VECTOR = 1
 
 
@@ -31,6 +30,7 @@ def tile_list_page_headpicks_scattered_pl_kernel(
     with ExitStack() as ctx:
         lists = ctx.enter_context(tc.tile_pool(name="lists", bufs=1))
         sb = ctx.enter_context(tc.tile_pool(name="sb", bufs=1))
+        relay = ctx.enter_context(tc.tile_pool(name="relay", bufs=1))
         psum = ctx.enter_context(tc.psum_pool(name="psum", bufs=1))
 
         def tile(shape, dtype, name, tag=None):
@@ -41,54 +41,52 @@ def tile_list_page_headpicks_scattered_pl_kernel(
         read_h = lists.tile([P, O // 16], U16, name="read_h")
         put_y = lists.tile([P, O // 16], U16, name="put_y")
 
-        xs_raw = tile([P, T], U8, "xs_raw")
-        ws_raw = tile([P, R + N], U8, "ws_raw")
-        planes = tile([P, R + J + N], U8, "planes")
+        xs_raw = relay.tile([P, T], U8, name="xs_raw", align_bytes=ALIGN, offset=4 * R - T // 2)
+        rows = tile([P, R + N + J + N], U8, "rows")
         nc.vector.memset(xs_raw[:].bitcast(I32), 0)
-        nc.vector.memset(ws_raw[:].bitcast(I32), 0)
-        nc.vector.memset(planes[:].bitcast(I32), 0)
+        nc.vector.memset(rows[:].bitcast(I32), 0)
+        ws_raw, wbs_raw = rows[:, 0:R], rows[:, R : R + N]
+        x_plane0, wb_plane0 = R + N, R + N + J
 
-        xw_raw = tile([P, T], I32, "xw_raw")
-        ww_raw = tile([P, R], I32, "ww_raw")
-        wbw_raw = tile([P, 2 * N], U8, "wbw_raw", tag="page2")
+        xw_raw = tile([P, T], I32, "xw_raw", tag="oldh")
+        ww_raw = tile([P, R], I32, "ww_raw", tag="wbw")
+        wbw_raw = tile([P, 2 * N], U8, "wbw_raw")
         nc.sync.dma_start(pick[:], offs)
         nc.scalar.dma_start(xs_raw[0:P:8, :].bitcast(I32), xt_scales[0].bitcast(I32))
-        nc.scalar.dma_start(ws_raw[0:P:8, 0:R].bitcast(I32), w_scales[0].bitcast(I32))
         nc.sync.dma_start(xw_raw[:], xt_words[0].rearrange("p c r -> p (c r)").bitcast(I32))
         nc.sync.dma_start(ww_raw[:], w_words[0].rearrange("p c r -> p (c r)").bitcast(I32))
+        for x in range(4):
+            nc.scalar.dma_start(rows[32 * x : 32 * x + 4, 0:R].bitcast(I32), w_scales[0, 4 * x : 4 * x + 4, :].bitcast(I32))
+        nc.sync.dma_start(wbw_raw[:].bitcast(I32), wb_words[0].bitcast(I32))
+        nc.gpsimd.dma_start(rows[0:P:8, R : R + N].bitcast(I32), wb_scales[0].bitcast(I32))
         nc.sync.dma_start(put_h[:], offs2)
         nc.sync.dma_start(read_h[:], offs3)
         nc.sync.dma_start(put_y[:], offs4)
-        nc.sync.dma_start(wbw_raw[:].bitcast(I32), wb_words[0].bitcast(I32))
-        nc.scalar.dma_start(ws_raw[0:P:8, R : R + N].bitcast(I32), wb_scales[0].bitcast(I32))
 
         placed_h = [None] * PACK
-        for t in range(2):
-            placed_h[t] = tile([P, C], F32, "placed_h%d" % t)
+        for t in range(PACK - 1):
+            placed_h[t] = tile([P, C], F32, "placed_h%d" % t, tag="page%d" % t)
             nc.vector.memset(placed_h[t][:], 0.0)
 
         xs_picked = tile([P, J], U8, "xs_picked")
         nc.vector.tensor_copy(xs_picked[:], xs_raw[:].indirect(pick[:]))
-        spread = tile([P, R + J], U8, "spread", tag="oldh")
-        nc.vector.tensor_copy(
-            spread[:, 0:R].rearrange("p (t m) -> p t m", t=PACK), ws_raw[:, 0:R].rearrange("p (m t) -> p t m", t=PACK)
-        )
-        nc.vector.tensor_copy(spread[:, R : R + J].bitcast(I32), xs_picked[:].bitcast(I32))
         for x in range(4):
             queue = nc.scalar if x % 2 == 0 else nc.sync
-            queue.dma_start(planes[32 * x : 32 * x + 4, 0 : R + J].bitcast(I32), spread[32 * x : 32 * x + 32 : 8, :].bitcast(I32))
+            queue.dma_start(
+                rows[32 * x : 32 * x + 4, x_plane0 : x_plane0 + J].bitcast(I32), xs_picked[32 * x : 32 * x + 32 : 8, :].bitcast(I32)
+            )
 
-        xw = tile([P, J], I32, "xw", tag="page3")
+        xw = relay.tile([P, J], I32, name="xw", align_bytes=ALIGN, offset=4 * R)
         nc.vector.tensor_copy(xw[:].bitcast(U32), xw_raw[:].bitcast(U32).indirect(pick[:]))
-        ww = tile([P, R], I32, "ww", tag="old")
+        ww = relay.tile([P, R], I32, name="ww", align_bytes=ALIGN, offset=0)
         nc.vector.tensor_copy(
             ww[:].rearrange("p (t c i) -> p c t i", t=PACK, i=4), ww_raw[:].rearrange("p (c i t) -> p c t i", t=PACK, i=4)
         )
+        w_plane = tile([P, R], U8, "w_plane")
+        nc.vector.tensor_copy(w_plane[:].rearrange("p (t m) -> p t m", t=PACK), ws_raw.rearrange("p (m t) -> p t m", t=PACK))
         spread_b = tile([P, N], U8, "spread_b")
-        nc.vector.tensor_copy(
-            spread_b[:].rearrange("p (t m) -> p t m", t=PACK), ws_raw[:, R : R + N].rearrange("p (m t) -> p t m", t=PACK)
-        )
-        wbw = tile([P, 2 * N], U8, "wbw")
+        nc.vector.tensor_copy(spread_b[:].rearrange("p (t m) -> p t m", t=PACK), wbs_raw.rearrange("p (m t) -> p t m", t=PACK))
+        wbw = tile([P, 2 * N], U8, "wbw", tag="wbw")
         nc.vector.tensor_copy(
             wbw[:].rearrange("p (t m b) -> p t m b", t=PACK, b=2), wbw_raw[:].rearrange("p (m t b) -> p t m b", t=PACK, b=2)
         )
@@ -99,24 +97,21 @@ def tile_list_page_headpicks_scattered_pl_kernel(
             nc.sync.dma_start(oldh_sb[:, t, :], oldh_rows[:, t, :])
         for x in range(4):
             nc.sync.dma_start(
-                planes[32 * x : 32 * x + 4, R + J : R + J + N].bitcast(I32), spread_b[32 * x : 32 * x + 32 : 8, :].bitcast(I32)
+                rows[32 * x : 32 * x + 4, wb_plane0 : wb_plane0 + N].bitcast(I32), spread_b[32 * x : 32 * x + 32 : 8, :].bitcast(I32)
             )
 
         a = [psum.tile([P, J], F32, name="a%d" % t) for t in range(PACK)]
         for t in range(PACK):
             cols = slice(t * P, (t + 1) * P)
             nc.tensor.matmul_mx(
-                a[t][:], lhsT=ww[:, cols].bitcast(E5M2), lhsT_scale=planes[:, cols],
-                rhs=xw[:].bitcast(E4M3), rhs_scale=planes[:, R : R + J], start=True, stop=True,
+                a[t][:], lhsT=ww[:, cols].bitcast(E5M2), lhsT_scale=w_plane[:, cols],
+                rhs=xw[:].bitcast(E4M3), rhs_scale=rows[:, x_plane0 : x_plane0 + J], start=True, stop=True,
             )
 
-        old_sb = tile([P, PACK, D], F32, "old_sb", tag="old")
+        old_sb = relay.tile([P, PACK, D], F32, name="old_sb", align_bytes=ALIGN, offset=0)
         old_rows = old.rearrange("(p t) d -> p t d", t=PACK)
         for u in range(2):
             nc.sync.dma_start(old_sb[:, 2 * u : 2 * u + 2, :], old_rows[:, 2 * u : 2 * u + 2, :])
-        for t in range(2, PACK):
-            placed_h[t] = tile([P, C], F32, "placed_h%d" % t, tag="page%d" % t)
-            nc.gpsimd.memset(placed_h[t][:], 0.0)
 
         def scatter(t, window, offsets, values):
             if t == ON_VECTOR:
@@ -131,33 +126,38 @@ def tile_list_page_headpicks_scattered_pl_kernel(
             else:
                 nc.vector.tensor_scalar_max(ha[t][:], a[t][:], 0.0)
         for t in range(PACK):
+            if t == PACK - 1:
+                placed_h[t] = tile([P, C], F32, "placed_h%d" % t, tag="ha%d" % ON_VECTOR)
+                nc.gpsimd.memset(placed_h[t][:], 0.0)
             scatter(t, placed_h[t], put_h, ha[t])
-        placed_y = []
-        for t in range(PACK):
-            placed_y.append(tile([P, D], F32, "placed_y%d" % t, tag="ha%d" % t))
-            nc.gpsimd.memset(placed_y[t][:], 0.0)
         pg = [tile([P, C], F32, "pg%d" % t) for t in range(PACK)]
         for t in range(PACK):
             nc.vector.tensor_tensor(pg[t][:], placed_h[t][:], oldh_sb[:, t, :], ALU.add)
-        hid = tile([P, PACK, O], BF16, "hid")
+        placed_y = []
+        for t in range(PACK - 1):
+            placed_y.append(tile([P, D], F32, "placed_y%d" % t, tag="page%d" % t))
+            nc.gpsimd.memset(placed_y[t][:], 0.0)
+        hid = tile([P, PACK, O], BF16, "hid", tag="ha3")
         for t in range(PACK):
             if t == PACK - 1:
                 nc.vector.tensor_copy(hid[:, t, :], pg[t][:].indirect(read_h[:]))
             else:
                 nc.scalar.activation(hid[:, t, :], pg[t][:].indirect(read_h[:]), ACT.Copy)
-        hid_grouped = tile([P, O, PACK], BF16, "hid_grouped")
+        hid_grouped = tile([P, O, PACK], BF16, "hid_grouped", tag="page3")
         nc.vector.tensor_copy(
             hid_grouped[:].rearrange("p (c i) t -> p c t i", i=4), hid[:].rearrange("p t (c i) -> p c t i", i=4)
         )
         hid_codes = tile([P, O], U32, "hid_codes")
         hid_scales = tile([P, O], U8, "hid_scales")
         nc.vector.quantize_mx(hid_codes[:].bitcast(E5M2), hid_scales[:], hid_grouped[:].rearrange("p o t -> p (o t)"))
+        placed_y.append(tile([P, D], F32, "placed_y3", tag="page3"))
+        nc.vector.memset(placed_y[PACK - 1][:], 0.0)
 
         prod = [psum.tile([P, O], F32, name="prod%d" % t) for t in range(PACK)]
         for t in range(PACK):
             nc.tensor.matmul_mx(
                 prod[t][:], lhsT=wbw[:, 2 * P * t : 2 * P * (t + 1)].bitcast(E2M1),
-                lhsT_scale=planes[:, R + J + P * t : R + J + P * (t + 1)],
+                lhsT_scale=rows[:, wb_plane0 + P * t : wb_plane0 + P * (t + 1)],
                 rhs=hid_codes[:].bitcast(E5M2), rhs_scale=hid_scales[:], start=True, stop=True,
             )
         p_sb = [tile([P, O], F32, "p_sb%d" % t) for t in range(PACK)]
@@ -172,7 +172,7 @@ def tile_list_page_headpicks_scattered_pl_kernel(
         y = tile([P, PACK, D], F32, "y")
         y_rows = out_0.rearrange("(p t) d -> p t d", t=PACK)
         for t in range(PACK):
-            pieces = [slice(0, HALF), slice(HALF, D)] if t == PACK - 1 else [slice(0, D)]
+            pieces = [slice(0, 256), slice(256, D)] if t == PACK - 1 else [slice(0, D)]
             for cols in pieces:
                 nc.vector.scalar_tensor_tensor(y[:, t, cols], old_sb[:, t, cols], 0.5, placed_y[t][:, cols], ALU.mult, ALU.add)
             nc.sync.dma_start(y_rows[:, t, :], y[:, t, :])
@@ -181,16 +181,16 @@ def tile_list_page_headpicks_scattered_pl_kernel(
         y_codes = tile([P, D], U32, "y_codes")
         y_scales = tile([P, D], U8, "y_scales")
         words_out = out_1[0].rearrange("p c r -> p (c r)").bitcast(I32)
-        for half in range(2):
-            cols = slice(half * HALF, (half + 1) * HALF)
+        on_scalar = [slice(0, 256), slice(256, 512), slice(512, 640)]
+        on_vector = slice(640, D)
+        for cols in on_scalar + [on_vector]:
             dst = y_grouped[:, cols, :].rearrange("p (c i) t -> p c t i", i=4)
             src = y[:, :, cols].rearrange("p t (c i) -> p c t i", i=4)
-            if half == 0:
-                nc.scalar.activation(dst, src, ACT.Copy)
-            else:
+            if cols == on_vector:
                 nc.vector.tensor_copy(dst, src)
-        for half in (1, 0):
-            cols = slice(half * HALF, (half + 1) * HALF)
+            else:
+                nc.scalar.activation(dst, src, ACT.Copy)
+        for cols in [on_scalar[0], on_vector] + on_scalar[1:]:
             nc.vector.quantize_mx(
                 y_codes[:, cols].bitcast(E4M3), y_scales[:, cols], y_grouped[:, cols, :].rearrange("p c t -> p (c t)")
             )

@@ -20,7 +20,7 @@ ALU = mybir.AluOpType
 P = 128
 PACK = 4
 ALIGN = 64
-ON_VECTOR = 1
+ON_VECTOR = 0
 
 
 def tile_list_page_headpicks_scattered_pl_kernel(
@@ -42,27 +42,36 @@ def tile_list_page_headpicks_scattered_pl_kernel(
         put_y = lists.tile([P, O // 16], U16, name="put_y")
 
         xs_raw = relay.tile([P, T], U8, name="xs_raw", align_bytes=ALIGN, offset=4 * R - T // 2)
-        rows = tile([P, R + N + J + N], U8, "rows")
-        nc.vector.memset(xs_raw[:].bitcast(I32), 0)
-        nc.vector.memset(rows[:].bitcast(I32), 0)
-        ws_raw, wbs_raw = rows[:, 0:R], rows[:, R : R + N]
-        x_plane0, wb_plane0 = R + N, R + N + J
-
+        ws_raw = tile([P, R], U8, "ws_raw")
+        wbs_raw = tile([P, N], U8, "wbs_raw")
         xw_raw = tile([P, T], I32, "xw_raw", tag="oldh")
         ww_raw = tile([P, R], I32, "ww_raw", tag="wbw")
         wbw_raw = tile([P, 2 * N], U8, "wbw_raw")
+
+        def block_rows(scales):
+            words = scales[0].bitcast(I32)
+            return words.unsqueeze(1).broadcast_to([16, 8, words.shape[1]])
+
         nc.sync.dma_start(pick[:], offs)
-        nc.scalar.dma_start(xs_raw[0:P:8, :].bitcast(I32), xt_scales[0].bitcast(I32))
+        nc.scalar.dma_start(xs_raw[:].bitcast(I32), block_rows(xt_scales))
         nc.sync.dma_start(xw_raw[:], xt_words[0].rearrange("p c r -> p (c r)").bitcast(I32))
         nc.sync.dma_start(ww_raw[:], w_words[0].rearrange("p c r -> p (c r)").bitcast(I32))
         for x in range(4):
-            nc.scalar.dma_start(rows[32 * x : 32 * x + 4, 0:R].bitcast(I32), w_scales[0, 4 * x : 4 * x + 4, :].bitcast(I32))
+            queue = nc.sync if x == 3 else nc.scalar
+            queue.dma_start(
+                ws_raw[32 * x : 32 * x + 32, :].bitcast(I32),
+                w_scales[0, 4 * x : 4 * x + 4, :].bitcast(I32).unsqueeze(0).broadcast_to([8, 4, R // 4]),
+            )
+        nc.gpsimd.dma_start(wbs_raw[:].bitcast(I32), block_rows(wb_scales))
         nc.sync.dma_start(wbw_raw[:].bitcast(I32), wb_words[0].bitcast(I32))
-        nc.gpsimd.dma_start(rows[0:P:8, R : R + N].bitcast(I32), wb_scales[0].bitcast(I32))
         nc.sync.dma_start(put_h[:], offs2)
         nc.sync.dma_start(read_h[:], offs3)
         nc.sync.dma_start(put_y[:], offs4)
 
+        x_plane = tile([P, J], U8, "x_plane")
+        nc.vector.memset(x_plane[:].bitcast(I32), 0)
+        wb_plane = tile([P, N], U8, "wb_plane")
+        nc.vector.memset(wb_plane[:].bitcast(I32), 0)
         placed_h = [None] * PACK
         for t in range(PACK - 1):
             placed_h[t] = tile([P, C], F32, "placed_h%d" % t, tag="page%d" % t)
@@ -73,7 +82,7 @@ def tile_list_page_headpicks_scattered_pl_kernel(
         for x in range(4):
             queue = nc.scalar if x % 2 == 0 else nc.sync
             queue.dma_start(
-                rows[32 * x : 32 * x + 4, x_plane0 : x_plane0 + J].bitcast(I32), xs_picked[32 * x : 32 * x + 32 : 8, :].bitcast(I32)
+                x_plane[32 * x : 32 * x + 4, :].bitcast(I32), xs_picked[32 * x : 32 * x + 32 : 8, :].bitcast(I32)
             )
 
         xw = relay.tile([P, J], I32, name="xw", align_bytes=ALIGN, offset=4 * R)
@@ -83,9 +92,9 @@ def tile_list_page_headpicks_scattered_pl_kernel(
             ww[:].rearrange("p (t c i) -> p c t i", t=PACK, i=4), ww_raw[:].rearrange("p (c i t) -> p c t i", t=PACK, i=4)
         )
         w_plane = tile([P, R], U8, "w_plane")
-        nc.vector.tensor_copy(w_plane[:].rearrange("p (t m) -> p t m", t=PACK), ws_raw.rearrange("p (m t) -> p t m", t=PACK))
-        spread_b = tile([P, N], U8, "spread_b")
-        nc.vector.tensor_copy(spread_b[:].rearrange("p (t m) -> p t m", t=PACK), wbs_raw.rearrange("p (m t) -> p t m", t=PACK))
+        nc.vector.tensor_copy(w_plane[:].rearrange("p (t m) -> p t m", t=PACK), ws_raw[:].rearrange("p (m t) -> p t m", t=PACK))
+        wbs = tile([P, N], U8, "wbs")
+        nc.vector.tensor_copy(wbs[:].rearrange("p (t m) -> p t m", t=PACK), wbs_raw[:].rearrange("p (m t) -> p t m", t=PACK))
         wbw = tile([P, 2 * N], U8, "wbw", tag="wbw")
         nc.vector.tensor_copy(
             wbw[:].rearrange("p (t m b) -> p t m b", t=PACK, b=2), wbw_raw[:].rearrange("p (m t b) -> p t m b", t=PACK, b=2)
@@ -96,16 +105,14 @@ def tile_list_page_headpicks_scattered_pl_kernel(
         for t in range(PACK):
             nc.sync.dma_start(oldh_sb[:, t, :], oldh_rows[:, t, :])
         for x in range(4):
-            nc.sync.dma_start(
-                rows[32 * x : 32 * x + 4, wb_plane0 : wb_plane0 + N].bitcast(I32), spread_b[32 * x : 32 * x + 32 : 8, :].bitcast(I32)
-            )
+            nc.sync.dma_start(wb_plane[32 * x : 32 * x + 4, :].bitcast(I32), wbs[32 * x : 32 * x + 32 : 8, :].bitcast(I32))
 
         a = [psum.tile([P, J], F32, name="a%d" % t) for t in range(PACK)]
         for t in range(PACK):
             cols = slice(t * P, (t + 1) * P)
             nc.tensor.matmul_mx(
                 a[t][:], lhsT=ww[:, cols].bitcast(E5M2), lhsT_scale=w_plane[:, cols],
-                rhs=xw[:].bitcast(E4M3), rhs_scale=rows[:, x_plane0 : x_plane0 + J], start=True, stop=True,
+                rhs=xw[:].bitcast(E4M3), rhs_scale=x_plane[:], start=True, stop=True,
             )
 
         old_sb = relay.tile([P, PACK, D], F32, name="old_sb", align_bytes=ALIGN, offset=0)
@@ -119,13 +126,13 @@ def tile_list_page_headpicks_scattered_pl_kernel(
             else:
                 nc.scalar.activation(window[:].indirect(offsets[:]), values[:], ACT.Copy)
 
-        ha = [tile([P, J], F32, "ha%d" % t, tag="ha%d" % t) for t in range(PACK)]
+        ha = [None] * PACK
         for t in range(PACK):
-            if t % 2 == 0:
+            ha[t] = tile([P, J], F32, "ha%d" % t, tag="ha%d" % t)
+            if t in (1, 2):
                 nc.scalar.activation(ha[t][:], a[t][:], ACT.Relu)
             else:
                 nc.vector.tensor_scalar_max(ha[t][:], a[t][:], 0.0)
-        for t in range(PACK):
             if t == PACK - 1:
                 placed_h[t] = tile([P, C], F32, "placed_h%d" % t, tag="ha%d" % ON_VECTOR)
                 nc.gpsimd.memset(placed_h[t][:], 0.0)
@@ -133,13 +140,13 @@ def tile_list_page_headpicks_scattered_pl_kernel(
         pg = [tile([P, C], F32, "pg%d" % t) for t in range(PACK)]
         for t in range(PACK):
             nc.vector.tensor_tensor(pg[t][:], placed_h[t][:], oldh_sb[:, t, :], ALU.add)
-        placed_y = []
+        placed_y = [None] * PACK
         for t in range(PACK - 1):
-            placed_y.append(tile([P, D], F32, "placed_y%d" % t, tag="page%d" % t))
+            placed_y[t] = tile([P, D], F32, "placed_y%d" % t, tag="page%d" % t)
             nc.gpsimd.memset(placed_y[t][:], 0.0)
         hid = tile([P, PACK, O], BF16, "hid", tag="ha3")
         for t in range(PACK):
-            if t == PACK - 1:
+            if t == PACK - 2:
                 nc.vector.tensor_copy(hid[:, t, :], pg[t][:].indirect(read_h[:]))
             else:
                 nc.scalar.activation(hid[:, t, :], pg[t][:].indirect(read_h[:]), ACT.Copy)
@@ -150,29 +157,29 @@ def tile_list_page_headpicks_scattered_pl_kernel(
         hid_codes = tile([P, O], U32, "hid_codes")
         hid_scales = tile([P, O], U8, "hid_scales")
         nc.vector.quantize_mx(hid_codes[:].bitcast(E5M2), hid_scales[:], hid_grouped[:].rearrange("p o t -> p (o t)"))
-        placed_y.append(tile([P, D], F32, "placed_y3", tag="page3"))
+        placed_y[PACK - 1] = tile([P, D], F32, "placed_y3", tag="page3")
         nc.vector.memset(placed_y[PACK - 1][:], 0.0)
 
         prod = [psum.tile([P, O], F32, name="prod%d" % t) for t in range(PACK)]
         for t in range(PACK):
             nc.tensor.matmul_mx(
                 prod[t][:], lhsT=wbw[:, 2 * P * t : 2 * P * (t + 1)].bitcast(E2M1),
-                lhsT_scale=rows[:, wb_plane0 + P * t : wb_plane0 + P * (t + 1)],
+                lhsT_scale=wb_plane[:, P * t : P * (t + 1)],
                 rhs=hid_codes[:].bitcast(E5M2), rhs_scale=hid_scales[:], start=True, stop=True,
             )
-        p_sb = [tile([P, O], F32, "p_sb%d" % t) for t in range(PACK)]
+        p_sb = [None] * PACK
         for t in range(PACK):
-            if t % 2 == 0:
+            p_sb[t] = tile([P, O], F32, "p_sb%d" % t)
+            if t in (1, 2):
                 nc.scalar.activation(p_sb[t][:], prod[t][:], ACT.Copy)
             else:
                 nc.vector.tensor_copy(p_sb[t][:], prod[t][:])
-        for t in range(PACK):
             scatter(t, placed_y[t], put_y, p_sb[t])
 
         y = tile([P, PACK, D], F32, "y")
         y_rows = out_0.rearrange("(p t) d -> p t d", t=PACK)
         for t in range(PACK):
-            pieces = [slice(0, 256), slice(256, D)] if t == PACK - 1 else [slice(0, D)]
+            pieces = [slice(384, 640), slice(0, 384), slice(640, D)] if t == PACK - 1 else [slice(0, D)]
             for cols in pieces:
                 nc.vector.scalar_tensor_tensor(y[:, t, cols], old_sb[:, t, cols], 0.5, placed_y[t][:, cols], ALU.mult, ALU.add)
             nc.sync.dma_start(y_rows[:, t, :], y[:, t, :])
@@ -181,8 +188,8 @@ def tile_list_page_headpicks_scattered_pl_kernel(
         y_codes = tile([P, D], U32, "y_codes")
         y_scales = tile([P, D], U8, "y_scales")
         words_out = out_1[0].rearrange("p c r -> p (c r)").bitcast(I32)
-        on_scalar = [slice(0, 256), slice(256, 512), slice(512, 640)]
-        on_vector = slice(640, D)
+        on_scalar = [slice(384, 640), slice(640, 896), slice(896, D)]
+        on_vector = slice(0, 384)
         for cols in on_scalar + [on_vector]:
             dst = y_grouped[:, cols, :].rearrange("p (c i) t -> p c t i", i=4)
             src = y[:, :, cols].rearrange("p t (c i) -> p c t i", i=4)
@@ -194,7 +201,9 @@ def tile_list_page_headpicks_scattered_pl_kernel(
             nc.vector.quantize_mx(
                 y_codes[:, cols].bitcast(E4M3), y_scales[:, cols], y_grouped[:, cols, :].rearrange("p c t -> p (c t)")
             )
-            nc.sync.dma_start(words_out[:, cols], y_codes[:, cols].bitcast(I32))
+            if cols != on_scalar[0]:
+                stored = slice(0, on_scalar[0].stop) if cols == on_vector else cols
+                nc.sync.dma_start(words_out[:, stored], y_codes[:, stored].bitcast(I32))
         for x in range(4):
             queue = nc.scalar if x % 2 == 0 else nc.sync
             queue.dma_start(out_2[0, 4 * x : 4 * x + 4, :].bitcast(I32), y_scales[32 * x : 32 * x + 4, :].bitcast(I32))

@@ -31,6 +31,7 @@ def tile_list_page_headpicks_scattered_pl_kernel(
         lists = ctx.enter_context(tc.tile_pool(name="lists", bufs=1))
         sb = ctx.enter_context(tc.tile_pool(name="sb", bufs=1))
         relay = ctx.enter_context(tc.tile_pool(name="relay", bufs=1))
+        pages = ctx.enter_context(tc.tile_pool(name="pages", bufs=1))
         psum = ctx.enter_context(tc.psum_pool(name="psum", bufs=1))
 
         def tile(shape, dtype, name, tag=None):
@@ -42,11 +43,11 @@ def tile_list_page_headpicks_scattered_pl_kernel(
         put_y = lists.tile([P, O // 16], U16, name="put_y")
 
         xs_raw = relay.tile([P, T], U8, name="xs_raw", align_bytes=ALIGN, offset=4 * R - T // 2)
-        ws_raw = tile([P, R], U8, "ws_raw")
-        wbs_raw = tile([P, N], U8, "wbs_raw")
+        ws_raw = tile([P, R], U8, "ws_raw", tag="wbs")
+        wbs_raw = tile([P, N], U8, "wbs_raw", tag="wbw")
         xw_raw = tile([P, T], I32, "xw_raw", tag="oldh")
-        ww_raw = tile([P, R], I32, "ww_raw", tag="wbw")
-        wbw_raw = tile([P, 2 * N], U8, "wbw_raw")
+        ww_raw = tile([P, R], I32, "ww_raw")
+        wbw_raw = pages.tile([P, 2 * N], U8, name="wbw_raw", align_bytes=ALIGN, offset=4 * D - N)
 
         def block_rows(scales):
             words = scales[0].bitcast(I32)
@@ -73,8 +74,8 @@ def tile_list_page_headpicks_scattered_pl_kernel(
         wb_plane = tile([P, N], U8, "wb_plane")
         nc.vector.memset(wb_plane[:].bitcast(I32), 0)
         placed_h = [None] * PACK
-        for t in range(PACK - 1):
-            placed_h[t] = tile([P, C], F32, "placed_h%d" % t, tag="page%d" % t)
+        for t in range(PACK):
+            placed_h[t] = tile([P, C], F32, "placed_h%d" % t)
             nc.vector.memset(placed_h[t][:], 0.0)
 
         xs_picked = tile([P, J], U8, "xs_picked")
@@ -93,12 +94,21 @@ def tile_list_page_headpicks_scattered_pl_kernel(
         )
         w_plane = tile([P, R], U8, "w_plane")
         nc.vector.tensor_copy(w_plane[:].rearrange("p (t m) -> p t m", t=PACK), ws_raw[:].rearrange("p (m t) -> p t m", t=PACK))
-        wbs = tile([P, N], U8, "wbs")
+        wbs = tile([P, N], U8, "wbs", tag="wbs")
         nc.vector.tensor_copy(wbs[:].rearrange("p (t m) -> p t m", t=PACK), wbs_raw[:].rearrange("p (m t) -> p t m", t=PACK))
         wbw = tile([P, 2 * N], U8, "wbw", tag="wbw")
         nc.vector.tensor_copy(
             wbw[:].rearrange("p (t m b) -> p t m b", t=PACK, b=2), wbw_raw[:].rearrange("p (m t b) -> p t m b", t=PACK, b=2)
         )
+
+        placed_y = [None] * PACK
+
+        def clear_pages(first):
+            for t in (first, first + 1):
+                placed_y[t] = pages.tile([P, D], F32, name="placed_y%d" % t, align_bytes=ALIGN, offset=4 * D * t)
+                nc.gpsimd.memset(placed_y[t][:], 0.0)
+
+        clear_pages(0)
 
         oldh_sb = tile([P, PACK, C], F32, "oldh_sb", tag="oldh")
         oldh_rows = oldh.rearrange("(p t) c -> p t c", t=PACK)
@@ -133,32 +143,24 @@ def tile_list_page_headpicks_scattered_pl_kernel(
                 nc.scalar.activation(ha[t][:], a[t][:], ACT.Relu)
             else:
                 nc.vector.tensor_scalar_max(ha[t][:], a[t][:], 0.0)
-            if t == PACK - 1:
-                placed_h[t] = tile([P, C], F32, "placed_h%d" % t, tag="ha%d" % ON_VECTOR)
-                nc.gpsimd.memset(placed_h[t][:], 0.0)
             scatter(t, placed_h[t], put_h, ha[t])
         pg = [tile([P, C], F32, "pg%d" % t) for t in range(PACK)]
         for t in range(PACK):
             nc.vector.tensor_tensor(pg[t][:], placed_h[t][:], oldh_sb[:, t, :], ALU.add)
-        placed_y = [None] * PACK
-        for t in range(PACK - 1):
-            placed_y[t] = tile([P, D], F32, "placed_y%d" % t, tag="page%d" % t)
-            nc.gpsimd.memset(placed_y[t][:], 0.0)
         hid = tile([P, PACK, O], BF16, "hid", tag="ha3")
         for t in range(PACK):
             if t == PACK - 2:
                 nc.vector.tensor_copy(hid[:, t, :], pg[t][:].indirect(read_h[:]))
             else:
                 nc.scalar.activation(hid[:, t, :], pg[t][:].indirect(read_h[:]), ACT.Copy)
-        hid_grouped = tile([P, O, PACK], BF16, "hid_grouped", tag="page3")
+        hid_grouped = pages.tile([P, O, PACK], BF16, name="hid_grouped", align_bytes=ALIGN, offset=3 * 4 * D - PACK * O)
         nc.vector.tensor_copy(
             hid_grouped[:].rearrange("p (c i) t -> p c t i", i=4), hid[:].rearrange("p t (c i) -> p c t i", i=4)
         )
         hid_codes = tile([P, O], U32, "hid_codes")
         hid_scales = tile([P, O], U8, "hid_scales")
         nc.vector.quantize_mx(hid_codes[:].bitcast(E5M2), hid_scales[:], hid_grouped[:].rearrange("p o t -> p (o t)"))
-        placed_y[PACK - 1] = tile([P, D], F32, "placed_y3", tag="page3")
-        nc.vector.memset(placed_y[PACK - 1][:], 0.0)
+        clear_pages(2)
 
         prod = [psum.tile([P, O], F32, name="prod%d" % t) for t in range(PACK)]
         for t in range(PACK):

@@ -19,8 +19,20 @@ ALU = mybir.AluOpType
 
 P = 128
 PACK = 4
+QUADS = 4
+BLOCK_PARTS = 8
+BLOCKS = P // BLOCK_PARTS
+LIST_PARTS = 16
 ALIGN = 64
-ON_VECTOR = 0
+LINE = 4
+PAGE_BYTES = 4 * D
+
+VECTOR_SCATTERS = 0
+VECTOR_GATHERS = 2
+SCALAR_EMPTIES = (1, 2)
+HID_SPLIT = 192
+VECTOR_WEAVES = slice(0, 384)
+SCALAR_WEAVES = [slice(384, 640), slice(640, 896), slice(896, D)]
 
 
 def tile_list_page_headpicks_scattered_pl_kernel(
@@ -37,28 +49,46 @@ def tile_list_page_headpicks_scattered_pl_kernel(
         def tile(shape, dtype, name, tag=None):
             return sb.tile(shape, dtype, name=name, tag=tag or name, align_bytes=ALIGN)
 
-        pick = lists.tile([P, J // 16], U16, name="pick")
-        put_h = lists.tile([P, J // 16], U16, name="put_h")
-        read_h = lists.tile([P, O // 16], U16, name="read_h")
-        put_y = lists.tile([P, O // 16], U16, name="put_y")
-
-        xs_raw = relay.tile([P, T], U8, name="xs_raw", align_bytes=ALIGN, offset=4 * R - T // 2)
-        ws_raw = tile([P, R], U8, "ws_raw", tag="wbs")
-        wbs_raw = tile([P, N], U8, "wbs_raw", tag="wbw")
-        xw_raw = tile([P, T], I32, "xw_raw", tag="oldh")
-        ww_raw = tile([P, R], I32, "ww_raw")
-        wbw_raw = pages.tile([P, 2 * N], U8, name="wbw_raw", align_bytes=ALIGN, offset=4 * D - N)
+        def tile_at(pool, offset, shape, dtype, name):
+            return pool.tile(shape, dtype, name=name, align_bytes=ALIGN, offset=offset)
 
         def block_rows(scales):
             words = scales[0].bitcast(I32)
-            return words.unsqueeze(1).broadcast_to([16, 8, words.shape[1]])
+            return words.unsqueeze(1).broadcast_to([BLOCKS, BLOCK_PARTS, words.shape[1]])
+
+        def rows_to_plane(queue, plane, rows, x):
+            queue.dma_start(plane[32 * x : 32 * x + 4, :].bitcast(I32), rows[32 * x : 32 * x + 32 : BLOCK_PARTS, :].bitcast(I32))
+
+        def deal(dealt, raw):
+            nc.vector.tensor_copy(dealt.rearrange("p (t m) -> p t m", t=PACK), raw.rearrange("p (m t) -> p t m", t=PACK))
+
+        def weave_views(woven, slices):
+            return woven.rearrange("p (c i) t -> p c t i", i=LINE), slices.rearrange("p t (c i) -> p c t i", i=LINE)
+
+        def scatter(t, window, offsets, values):
+            if t == VECTOR_SCATTERS:
+                nc.vector.tensor_copy(window[:].indirect(offsets[:]), values[:])
+            else:
+                nc.scalar.activation(window[:].indirect(offsets[:]), values[:], ACT.Copy)
+
+        pick = lists.tile([P, J // LIST_PARTS], U16, name="pick")
+        put_h = lists.tile([P, J // LIST_PARTS], U16, name="put_h")
+        read_h = lists.tile([P, O // LIST_PARTS], U16, name="read_h")
+        put_y = lists.tile([P, O // LIST_PARTS], U16, name="put_y")
+
+        xs_raw = tile_at(relay, 4 * R - T // 2, [P, T], U8, "xs_raw")
+        ws_raw = tile([P, R], U8, "ws_raw", tag="wbw")
+        wbw_raw = tile([P, 2 * N], U8, "wbw_raw", tag="wbs")
+        xw_raw = tile([P, T], I32, "xw_raw", tag="oldh")
+        ww_raw = tile([P, R], I32, "ww_raw")
+        wbs_raw = tile_at(pages, PAGE_BYTES - N // 2, [P, N], U8, "wbs_raw")
 
         nc.sync.dma_start(pick[:], offs)
         nc.scalar.dma_start(xs_raw[:].bitcast(I32), block_rows(xt_scales))
         nc.sync.dma_start(xw_raw[:], xt_words[0].rearrange("p c r -> p (c r)").bitcast(I32))
         nc.sync.dma_start(ww_raw[:], w_words[0].rearrange("p c r -> p (c r)").bitcast(I32))
-        for x in range(4):
-            queue = nc.sync if x == 3 else nc.scalar
+        for x in range(QUADS):
+            queue = nc.sync if x == QUADS - 1 else nc.scalar
             queue.dma_start(
                 ws_raw[32 * x : 32 * x + 32, :].bitcast(I32),
                 w_scales[0, 4 * x : 4 * x + 4, :].bitcast(I32).unsqueeze(0).broadcast_to([8, 4, R // 4]),
@@ -80,32 +110,27 @@ def tile_list_page_headpicks_scattered_pl_kernel(
 
         xs_picked = tile([P, J], U8, "xs_picked")
         nc.vector.tensor_copy(xs_picked[:], xs_raw[:].indirect(pick[:]))
-        for x in range(4):
-            queue = nc.scalar if x % 2 == 0 else nc.sync
-            queue.dma_start(
-                x_plane[32 * x : 32 * x + 4, :].bitcast(I32), xs_picked[32 * x : 32 * x + 32 : 8, :].bitcast(I32)
-            )
-
-        xw = relay.tile([P, J], I32, name="xw", align_bytes=ALIGN, offset=4 * R)
+        for x in range(QUADS):
+            rows_to_plane(nc.scalar if x % 2 == 0 else nc.sync, x_plane, xs_picked, x)
+        xw = tile_at(relay, 4 * R, [P, J], I32, "xw")
         nc.vector.tensor_copy(xw[:].bitcast(U32), xw_raw[:].bitcast(U32).indirect(pick[:]))
-        ww = relay.tile([P, R], I32, name="ww", align_bytes=ALIGN, offset=0)
+
+        ww = tile_at(relay, 0, [P, R], I32, "ww")
         nc.vector.tensor_copy(
-            ww[:].rearrange("p (t c i) -> p c t i", t=PACK, i=4), ww_raw[:].rearrange("p (c i t) -> p c t i", t=PACK, i=4)
+            ww[:].rearrange("p (t c i) -> p c t i", t=PACK, i=LINE), ww_raw[:].rearrange("p (c i t) -> p c t i", t=PACK, i=LINE)
         )
         w_plane = tile([P, R], U8, "w_plane")
-        nc.vector.tensor_copy(w_plane[:].rearrange("p (t m) -> p t m", t=PACK), ws_raw[:].rearrange("p (m t) -> p t m", t=PACK))
-        wbs = tile([P, N], U8, "wbs", tag="wbs")
-        nc.vector.tensor_copy(wbs[:].rearrange("p (t m) -> p t m", t=PACK), wbs_raw[:].rearrange("p (m t) -> p t m", t=PACK))
+        deal(w_plane[:], ws_raw[:])
         wbw = tile([P, 2 * N], U8, "wbw", tag="wbw")
-        nc.vector.tensor_copy(
-            wbw[:].rearrange("p (t m b) -> p t m b", t=PACK, b=2), wbw_raw[:].rearrange("p (m t b) -> p t m b", t=PACK, b=2)
-        )
+        deal(wbw[:].bitcast(U16), wbw_raw[:].bitcast(U16))
+        wbs = tile([P, N], U8, "wbs", tag="wbs")
+        deal(wbs[:], wbs_raw[:])
 
         placed_y = [None] * PACK
 
         def clear_pages(first):
             for t in (first, first + 1):
-                placed_y[t] = pages.tile([P, D], F32, name="placed_y%d" % t, align_bytes=ALIGN, offset=4 * D * t)
+                placed_y[t] = tile_at(pages, PAGE_BYTES * t, [P, D], F32, "placed_y%d" % t)
                 nc.gpsimd.memset(placed_y[t][:], 0.0)
 
         clear_pages(0)
@@ -114,8 +139,8 @@ def tile_list_page_headpicks_scattered_pl_kernel(
         oldh_rows = oldh.rearrange("(p t) c -> p t c", t=PACK)
         for t in range(PACK):
             nc.sync.dma_start(oldh_sb[:, t, :], oldh_rows[:, t, :])
-        for x in range(4):
-            nc.sync.dma_start(wb_plane[32 * x : 32 * x + 4, :].bitcast(I32), wbs[32 * x : 32 * x + 32 : 8, :].bitcast(I32))
+        for x in range(QUADS):
+            rows_to_plane(nc.sync, wb_plane, wbs, x)
 
         a = [psum.tile([P, J], F32, name="a%d" % t) for t in range(PACK)]
         for t in range(PACK):
@@ -125,21 +150,15 @@ def tile_list_page_headpicks_scattered_pl_kernel(
                 rhs=xw[:].bitcast(E4M3), rhs_scale=x_plane[:], start=True, stop=True,
             )
 
-        old_sb = relay.tile([P, PACK, D], F32, name="old_sb", align_bytes=ALIGN, offset=0)
+        old_sb = tile_at(relay, 0, [P, PACK, D], F32, "old_sb")
         old_rows = old.rearrange("(p t) d -> p t d", t=PACK)
         for u in range(2):
             nc.sync.dma_start(old_sb[:, 2 * u : 2 * u + 2, :], old_rows[:, 2 * u : 2 * u + 2, :])
 
-        def scatter(t, window, offsets, values):
-            if t == ON_VECTOR:
-                nc.vector.tensor_copy(window[:].indirect(offsets[:]), values[:])
-            else:
-                nc.scalar.activation(window[:].indirect(offsets[:]), values[:], ACT.Copy)
-
         ha = [None] * PACK
         for t in range(PACK):
-            ha[t] = tile([P, J], F32, "ha%d" % t, tag="ha%d" % t)
-            if t in (1, 2):
+            ha[t] = tile([P, J], F32, "ha%d" % t)
+            if t in SCALAR_EMPTIES:
                 nc.scalar.activation(ha[t][:], a[t][:], ACT.Relu)
             else:
                 nc.vector.tensor_scalar_max(ha[t][:], a[t][:], 0.0)
@@ -147,19 +166,18 @@ def tile_list_page_headpicks_scattered_pl_kernel(
         pg = [tile([P, C], F32, "pg%d" % t) for t in range(PACK)]
         for t in range(PACK):
             nc.vector.tensor_tensor(pg[t][:], placed_h[t][:], oldh_sb[:, t, :], ALU.add)
-        hid = tile([P, PACK, O], BF16, "hid", tag="ha3")
+        hid = tile([P, PACK, O], BF16, "hid", tag="ha%d" % (PACK - 1))
         for t in range(PACK):
-            if t == PACK - 2:
+            if t == VECTOR_GATHERS:
                 nc.vector.tensor_copy(hid[:, t, :], pg[t][:].indirect(read_h[:]))
             else:
                 nc.scalar.activation(hid[:, t, :], pg[t][:].indirect(read_h[:]), ACT.Copy)
-        hid_grouped = pages.tile([P, O, PACK], BF16, name="hid_grouped", align_bytes=ALIGN, offset=3 * 4 * D - PACK * O)
-        nc.vector.tensor_copy(
-            hid_grouped[:].rearrange("p (c i) t -> p c t i", i=4), hid[:].rearrange("p t (c i) -> p c t i", i=4)
-        )
+        hid_woven = tile_at(pages, 3 * PAGE_BYTES - PACK * O, [P, O, PACK], BF16, "hid_woven")
+        nc.vector.tensor_copy(*weave_views(hid_woven[:, :HID_SPLIT, :], hid[:, :, :HID_SPLIT]))
+        nc.scalar.activation(*weave_views(hid_woven[:, HID_SPLIT:, :], hid[:, :, HID_SPLIT:]), ACT.Copy)
         hid_codes = tile([P, O], U32, "hid_codes")
-        hid_scales = tile([P, O], U8, "hid_scales")
-        nc.vector.quantize_mx(hid_codes[:].bitcast(E5M2), hid_scales[:], hid_grouped[:].rearrange("p o t -> p (o t)"))
+        hid_plane = tile([P, O], U8, "hid_plane")
+        nc.vector.quantize_mx(hid_codes[:].bitcast(E5M2), hid_plane[:], hid_woven[:].rearrange("p o t -> p (o t)"))
         clear_pages(2)
 
         prod = [psum.tile([P, O], F32, name="prod%d" % t) for t in range(PACK)]
@@ -167,45 +185,47 @@ def tile_list_page_headpicks_scattered_pl_kernel(
             nc.tensor.matmul_mx(
                 prod[t][:], lhsT=wbw[:, 2 * P * t : 2 * P * (t + 1)].bitcast(E2M1),
                 lhsT_scale=wb_plane[:, P * t : P * (t + 1)],
-                rhs=hid_codes[:].bitcast(E5M2), rhs_scale=hid_scales[:], start=True, stop=True,
+                rhs=hid_codes[:].bitcast(E5M2), rhs_scale=hid_plane[:], start=True, stop=True,
             )
         p_sb = [None] * PACK
         for t in range(PACK):
             p_sb[t] = tile([P, O], F32, "p_sb%d" % t)
-            if t in (1, 2):
+            if t in SCALAR_EMPTIES:
                 nc.scalar.activation(p_sb[t][:], prod[t][:], ACT.Copy)
             else:
                 nc.vector.tensor_copy(p_sb[t][:], prod[t][:])
             scatter(t, placed_y[t], put_y, p_sb[t])
 
+        last_pieces = [SCALAR_WEAVES[0], VECTOR_WEAVES, slice(SCALAR_WEAVES[1].start, D)]
         y = tile([P, PACK, D], F32, "y")
         y_rows = out_0.rearrange("(p t) d -> p t d", t=PACK)
         for t in range(PACK):
-            pieces = [slice(384, 640), slice(0, 384), slice(640, D)] if t == PACK - 1 else [slice(0, D)]
-            for cols in pieces:
+            for cols in last_pieces if t == PACK - 1 else [slice(0, D)]:
                 nc.vector.scalar_tensor_tensor(y[:, t, cols], old_sb[:, t, cols], 0.5, placed_y[t][:, cols], ALU.mult, ALU.add)
             nc.sync.dma_start(y_rows[:, t, :], y[:, t, :])
 
-        y_grouped = tile([P, D, PACK], BF16, "y_grouped")
+        y_woven = tile([P, D, PACK], BF16, "y_woven")
         y_codes = tile([P, D], U32, "y_codes")
-        y_scales = tile([P, D], U8, "y_scales")
+        y_plane = tile([P, D], U8, "y_plane")
         words_out = out_1[0].rearrange("p c r -> p (c r)").bitcast(I32)
-        on_scalar = [slice(384, 640), slice(640, 896), slice(896, D)]
-        on_vector = slice(0, 384)
-        for cols in on_scalar + [on_vector]:
-            dst = y_grouped[:, cols, :].rearrange("p (c i) t -> p c t i", i=4)
-            src = y[:, :, cols].rearrange("p t (c i) -> p c t i", i=4)
-            if cols == on_vector:
-                nc.vector.tensor_copy(dst, src)
-            else:
-                nc.scalar.activation(dst, src, ACT.Copy)
-        for cols in [on_scalar[0], on_vector] + on_scalar[1:]:
+        for cols in SCALAR_WEAVES:
+            nc.scalar.activation(*weave_views(y_woven[:, cols, :], y[:, :, cols]), ACT.Copy)
+        nc.vector.tensor_copy(*weave_views(y_woven[:, VECTOR_WEAVES, :], y[:, :, VECTOR_WEAVES]))
+
+        def quantise_y(cols):
             nc.vector.quantize_mx(
-                y_codes[:, cols].bitcast(E4M3), y_scales[:, cols], y_grouped[:, cols, :].rearrange("p c t -> p (c t)")
+                y_codes[:, cols].bitcast(E4M3), y_plane[:, cols], y_woven[:, cols, :].rearrange("p c t -> p (c t)")
             )
-            if cols != on_scalar[0]:
-                stored = slice(0, on_scalar[0].stop) if cols == on_vector else cols
-                nc.sync.dma_start(words_out[:, stored], y_codes[:, stored].bitcast(I32))
-        for x in range(4):
+
+        def store_words(cols):
+            nc.sync.dma_start(words_out[:, cols], y_codes[:, cols].bitcast(I32))
+
+        quantise_y(SCALAR_WEAVES[0])
+        quantise_y(VECTOR_WEAVES)
+        store_words(slice(0, SCALAR_WEAVES[0].stop))
+        for cols in SCALAR_WEAVES[1:]:
+            quantise_y(cols)
+            store_words(cols)
+        for x in range(QUADS):
             queue = nc.scalar if x % 2 == 0 else nc.sync
-            queue.dma_start(out_2[0, 4 * x : 4 * x + 4, :].bitcast(I32), y_scales[32 * x : 32 * x + 4, :].bitcast(I32))
+            queue.dma_start(out_2[0, 4 * x : 4 * x + 4, :].bitcast(I32), y_plane[32 * x : 32 * x + 4, :].bitcast(I32))

from contextlib import ExitStack

import concourse.mybir as mybir

K, T, J, R, C, O, N, D = 512, 512, 256, 512, 1024, 256, 512, 1024
FLOPS = 2 * K * R * J + 2 * R * N * O

F32 = mybir.dt.float32
BF16 = mybir.dt.bfloat16
I32 = mybir.dt.int32
U32 = mybir.dt.uint32
U16 = mybir.dt.uint16
U8 = mybir.dt.uint8
E4M3 = mybir.dt.float8_e4m3fn_x4
E5M2 = mybir.dt.float8_e5m2_x4
E2M1 = mybir.dt.float4_e2m1fn_x4
ACT = mybir.ActivationFunctionType
ALU = mybir.AluOpType

P = 128
PACK = 4
QUADS = 4
BLOCK_PARTS = 8
BLOCKS = P // BLOCK_PARTS
LIST_PARTS = 16
ALIGN = 64
LINE = 4
PAGE_BYTES = 4 * D

VECTOR_SCATTERS = 0
VECTOR_GATHERS = 2
SCALAR_EMPTIES = (1, 2)
HID_SPLIT = 192
VECTOR_WEAVES = slice(0, 384)
SCALAR_WEAVES = [slice(384, 640), slice(640, 896), slice(896, D)]


def tile_list_page_headpicks_scattered_pl_kernel(
    tc, xt_words, xt_scales, w_words, w_scales, oldh, wb_words, wb_scales, old, offs, offs2, offs3, offs4, out_0, out_1, out_2
):
    nc = tc.nc
    with ExitStack() as ctx:
        lists = ctx.enter_context(tc.tile_pool(name="lists", bufs=1))
        sb = ctx.enter_context(tc.tile_pool(name="sb", bufs=1))
        relay = ctx.enter_context(tc.tile_pool(name="relay", bufs=1))
        pages = ctx.enter_context(tc.tile_pool(name="pages", bufs=1))
        psum = ctx.enter_context(tc.psum_pool(name="psum", bufs=1))

        def tile(shape, dtype, name, tag=None):
            return sb.tile(shape, dtype, name=name, tag=tag or name, align_bytes=ALIGN)

        def tile_at(pool, offset, shape, dtype, name):
            return pool.tile(shape, dtype, name=name, align_bytes=ALIGN, offset=offset)

        def block_rows(scales):
            words = scales[0].bitcast(I32)
            return words.unsqueeze(1).broadcast_to([BLOCKS, BLOCK_PARTS, words.shape[1]])

        def rows_to_plane(queue, plane, rows, x):
            queue.dma_start(plane[32 * x : 32 * x + 4, :].bitcast(I32), rows[32 * x : 32 * x + 32 : BLOCK_PARTS, :].bitcast(I32))

        def deal(dealt, raw):
            nc.vector.tensor_copy(dealt.rearrange("p (t m) -> p t m", t=PACK), raw.rearrange("p (m t) -> p t m", t=PACK))

        def weave_views(woven, slices):
            return woven.rearrange("p (c i) t -> p c t i", i=LINE), slices.rearrange("p t (c i) -> p c t i", i=LINE)

        def scatter(t, window, offsets, values):
            if t == VECTOR_SCATTERS:
                nc.vector.tensor_copy(window[:].indirect(offsets[:]), values[:])
            else:
                nc.scalar.activation(window[:].indirect(offsets[:]), values[:], ACT.Copy)

        pick = lists.tile([P, J // LIST_PARTS], U16, name="pick")
        put_h = lists.tile([P, J // LIST_PARTS], U16, name="put_h")
        read_h = lists.tile([P, O // LIST_PARTS], U16, name="read_h")
        put_y = lists.tile([P, O // LIST_PARTS], U16, name="put_y")

        xs_raw = tile_at(relay, 4 * R - T // 2, [P, T], U8, "xs_raw")
        ws_raw = tile([P, R], U8, "ws_raw", tag="wbw")
        wbw_raw = tile([P, 2 * N], U8, "wbw_raw", tag="wbs")
        xw_raw = tile([P, T], I32, "xw_raw", tag="oldh")
        ww_raw = tile([P, R], I32, "ww_raw")
        wbs_raw = tile_at(pages, PAGE_BYTES - N // 2, [P, N], U8, "wbs_raw")

        nc.sync.dma_start(pick[:], offs)
        nc.scalar.dma_start(xs_raw[:].bitcast(I32), block_rows(xt_scales))
        nc.sync.dma_start(xw_raw[:], xt_words[0].rearrange("p c r -> p (c r)").bitcast(I32))
        nc.sync.dma_start(ww_raw[:], w_words[0].rearrange("p c r -> p (c r)").bitcast(I32))
        for x in range(QUADS):
            queue = nc.sync if x == QUADS - 1 else nc.scalar
            queue.dma_start(
                ws_raw[32 * x : 32 * x + 32, :].bitcast(I32),
                w_scales[0, 4 * x : 4 * x + 4, :].bitcast(I32).unsqueeze(0).broadcast_to([8, 4, R // 4]),
            )
        nc.gpsimd.dma_start(wbs_raw[:].bitcast(I32), block_rows(wb_scales))
        nc.sync.dma_start(wbw_raw[:].bitcast(I32), wb_words[0].bitcast(I32))
        nc.sync.dma_start(put_h[:], offs2)
        nc.sync.dma_start(read_h[:], offs3)
        nc.sync.dma_start(put_y[:], offs4)

        x_plane = tile([P, J], U8, "x_plane")
        nc.vector.memset(x_plane[:].bitcast(I32), 0)
        wb_plane = tile([P, N], U8, "wb_plane")
        nc.vector.memset(wb_plane[:].bitcast(I32), 0)
        placed_h = [None] * PACK
        for t in range(PACK):
            placed_h[t] = tile([P, C], F32, "placed_h%d" % t)
            nc.vector.memset(placed_h[t][:], 0.0)

        xs_picked = tile([P, J], U8, "xs_picked")
        nc.vector.tensor_copy(xs_picked[:], xs_raw[:].indirect(pick[:]))
        for x in range(QUADS):
            rows_to_plane(nc.scalar if x % 2 == 0 else nc.sync, x_plane, xs_picked, x)
        xw = tile_at(relay, 4 * R, [P, J], I32, "xw")
        nc.vector.tensor_copy(xw[:].bitcast(U32), xw_raw[:].bitcast(U32).indirect(pick[:]))

        ww = tile_at(relay, 0, [P, R], I32, "ww")
        nc.vector.tensor_copy(
            ww[:].rearrange("p (t c i) -> p c t i", t=PACK, i=LINE), ww_raw[:].rearrange("p (c i t) -> p c t i", t=PACK, i=LINE)
        )
        w_plane = tile([P, R], U8, "w_plane")
        deal(w_plane[:], ws_raw[:])
        wbw = tile([P, 2 * N], U8, "wbw", tag="wbw")
        deal(wbw[:].bitcast(U16), wbw_raw[:].bitcast(U16))
        wbs = tile([P, N], U8, "wbs", tag="wbs")
        deal(wbs[:], wbs_raw[:])

        placed_y = [None] * PACK

        def clear_pages(first):
            for t in (first, first + 1):
                placed_y[t] = tile_at(pages, PAGE_BYTES * t, [P, D], F32, "placed_y%d" % t)
                nc.gpsimd.memset(placed_y[t][:], 0.0)

        clear_pages(0)

        oldh_sb = tile([P, PACK, C], F32, "oldh_sb", tag="oldh")
        oldh_rows = oldh.rearrange("(p t) c -> p t c", t=PACK)
        for t in range(PACK):
            nc.sync.dma_start(oldh_sb[:, t, :], oldh_rows[:, t, :])
        for x in range(QUADS):
            rows_to_plane(nc.sync, wb_plane, wbs, x)

        a = [psum.tile([P, J], F32, name="a%d" % t) for t in range(PACK)]
        for t in range(PACK):
            cols = slice(t * P, (t + 1) * P)
            nc.tensor.matmul_mx(
                a[t][:], lhsT=ww[:, cols].bitcast(E5M2), lhsT_scale=w_plane[:, cols],
                rhs=xw[:].bitcast(E4M3), rhs_scale=x_plane[:], start=True, stop=True,
            )

        old_sb = tile_at(relay, 0, [P, PACK, D], F32, "old_sb")
        old_rows = old.rearrange("(p t) d -> p t d", t=PACK)
        for u in range(2):
            nc.sync.dma_start(old_sb[:, 2 * u : 2 * u + 2, :], old_rows[:, 2 * u : 2 * u + 2, :])

        ha = [None] * PACK
        for t in range(PACK):
            ha[t] = tile([P, J], F32, "ha%d" % t)
            if t in SCALAR_EMPTIES:
                nc.scalar.activation(ha[t][:], a[t][:], ACT.Relu)
            else:
                nc.vector.tensor_scalar_max(ha[t][:], a[t][:], 0.0)
            scatter(t, placed_h[t], put_h, ha[t])
        pg = [tile([P, C], F32, "pg%d" % t) for t in range(PACK)]
        for t in range(PACK):
            nc.vector.tensor_tensor(pg[t][:], placed_h[t][:], oldh_sb[:, t, :], ALU.add)
        hid = tile([P, PACK, O], BF16, "hid", tag="ha%d" % (PACK - 1))
        for t in range(PACK):
            if t == VECTOR_GATHERS:
                nc.vector.tensor_copy(hid[:, t, :], pg[t][:].indirect(read_h[:]))
            else:
                nc.scalar.activation(hid[:, t, :], pg[t][:].indirect(read_h[:]), ACT.Copy)
        hid_woven = tile_at(pages, 3 * PAGE_BYTES - PACK * O, [P, O, PACK], BF16, "hid_woven")
        nc.vector.tensor_copy(*weave_views(hid_woven[:, :HID_SPLIT, :], hid[:, :, :HID_SPLIT]))
        nc.scalar.activation(*weave_views(hid_woven[:, HID_SPLIT:, :], hid[:, :, HID_SPLIT:]), ACT.Copy)
        hid_codes = tile([P, O], U32, "hid_codes")
        hid_plane = tile([P, O], U8, "hid_plane")
        nc.vector.quantize_mx(hid_codes[:].bitcast(E5M2), hid_plane[:], hid_woven[:].rearrange("p o t -> p (o t)"))
        clear_pages(2)

        prod = [psum.tile([P, O], F32, name="prod%d" % t) for t in range(PACK)]
        for t in range(PACK):
            nc.tensor.matmul_mx(
                prod[t][:], lhsT=wbw[:, 2 * P * t : 2 * P * (t + 1)].bitcast(E2M1),
                lhsT_scale=wb_plane[:, P * t : P * (t + 1)],
                rhs=hid_codes[:].bitcast(E5M2), rhs_scale=hid_plane[:], start=True, stop=True,
            )
        p_sb = [None] * PACK
        for t in range(PACK):
            p_sb[t] = tile([P, O], F32, "p_sb%d" % t)
            if t in SCALAR_EMPTIES:
                nc.scalar.activation(p_sb[t][:], prod[t][:], ACT.Copy)
            else:
                nc.vector.tensor_copy(p_sb[t][:], prod[t][:])
            scatter(t, placed_y[t], put_y, p_sb[t])

        last_pieces = [SCALAR_WEAVES[0], VECTOR_WEAVES, slice(SCALAR_WEAVES[1].start, D)]
        y = tile([P, PACK, D], F32, "y")
        y_rows = out_0.rearrange("(p t) d -> p t d", t=PACK)
        for t in range(PACK):
            for cols in last_pieces if t == PACK - 1 else [slice(0, D)]:
                nc.vector.scalar_tensor_tensor(y[:, t, cols], old_sb[:, t, cols], 0.5, placed_y[t][:, cols], ALU.mult, ALU.add)
            nc.sync.dma_start(y_rows[:, t, :], y[:, t, :])

        y_woven = tile([P, D, PACK], BF16, "y_woven")
        y_codes = tile([P, D], U32, "y_codes")
        y_plane = tile([P, D], U8, "y_plane")
        words_out = out_1[0].rearrange("p c r -> p (c r)").bitcast(I32)
        for cols in SCALAR_WEAVES:
            nc.scalar.activation(*weave_views(y_woven[:, cols, :], y[:, :, cols]), ACT.Copy)
        nc.vector.tensor_copy(*weave_views(y_woven[:, VECTOR_WEAVES, :], y[:, :, VECTOR_WEAVES]))

        def quantise_y(cols):
            nc.vector.quantize_mx(
                y_codes[:, cols].bitcast(E4M3), y_plane[:, cols], y_woven[:, cols, :].rearrange("p c t -> p (c t)")
            )

        def store_words(cols):
            nc.sync.dma_start(words_out[:, cols], y_codes[:, cols].bitcast(I32))

        quantise_y(SCALAR_WEAVES[0])
        quantise_y(VECTOR_WEAVES)
        store_words(slice(0, SCALAR_WEAVES[0].stop))
        for cols in SCALAR_WEAVES[1:]:
            quantise_y(cols)
            store_words(cols)
        for x in range(QUADS):
            queue = nc.scalar if x % 2 == 0 else nc.sync
            queue.dma_start(out_2[0, 4 * x : 4 * x + 4, :].bitcast(I32), y_plane[32 * x : 32 * x + 4, :].bitcast(I32))
